import numpy as np, ml_dtypes
CORES = [13,21,141,149]
N = 4
import mx_ref
NC, G = 128, 4
C = np.float32(0.00048828125)
BF = ml_dtypes.bfloat16
def cut(t, i, w=512):
    return t[:, w * i:w * i + w]
def tile(rs):
    return np.stack(rs, axis=2).reshape(128, -1).astype(BF)
def layer(w, X):
    out = []
    for i in range(G):
        for t in range(len(X)):
            p = mx_ref.matmul(mx_ref.quantize(cut(w, len(X) * i + t)), X[t])
            z = p if t == 0 else z + p
        out.append(z)
    return out
def gate(U, V):
    return [(np.maximum(u, 0) * v) * C for u, v in zip(U, V)]
def setup_inputs(rng):
    def f(*shape):
        return mx_ref.flush((rng.standard_normal(shape, dtype=np.float32) * np.exp2(rng.integers(-2, 3, shape[:-1] + (1,)))).astype(BF))
    return {"x": f(N, 128, 4 * NC), "u": f(N, 128, G * 512), "v": f(N, 128, G * 512), "w2": f(N, 128, N * 512)}
def setup_inputs_blocks(rng):
    d = setup_inputs(rng)
    for k in ("x", "u", "v", "w2"): d[k] = mx_ref.spread(d[k], rng, 2)
    return d
def setup_inputs_wide(rng):
    d = setup_inputs(rng)
    for k in ("x", "u", "v", "w2"): d[k] = mx_ref.flush((d[k].astype(np.float32) * np.exp2(rng.integers(-5, 6, (N, 1, 1))).astype(np.float32)).astype(BF))
    return d
def setup_inputs_zeros(rng):
    d = setup_inputs(rng); v = d["x"].reshape(N, 128, -1, 4).copy()
    v[np.broadcast_to((rng.random((N, 1, v.shape[2], 1)) < 0.33), v.shape)] = 0
    d["x"] = v.reshape(d["x"].shape)
    return d
def reference(x, u, v, w2):
    h = np.zeros((N, 128, 4 * NC), BF)
    for j in range(N):
        X = [mx_ref.quantize(x[j])]
        h[j] = tile(gate(layer(u[j], X), layer(v[j], X)))
    H = [mx_ref.quantize(h[j]) for j in range(N)]
    y = np.zeros((N, 128, NC), np.float32)
    for r in range(N):
        for j in range(N):
            p = mx_ref.matmul(mx_ref.quantize(cut(w2[r], j)), H[j])
            y[r] = p if j == 0 else y[r] + p
    return {"y": y}

from concourse.bass import DstId, RemoteDMATransfer
from concourse.mybir import dt, AluOpType, ActivationFunctionType

N = 4
G = 4
W = 128
E = 4 * W
BANK = 512
C = 0.00048828125
HOSTS = 2

SCRATCH = {
    "xb": ("sbuf", [128, E], "bfloat16"),
    "ub": ("sbuf", [128, G * E], "bfloat16"),
    "vb": ("sbuf", [128, G * E], "bfloat16"),
    "wb": ("sbuf", [128, N * E], "bfloat16"),
    "xq": ("sbuf", [128, W], "float8_e4m3fn_x4"),
    "xs": ("sbuf", [128, W], "uint8"),
    "uq": ("sbuf", [128, G * W], "float8_e4m3fn_x4"),
    "us": ("sbuf", [128, G * W], "uint8"),
    "vq": ("sbuf", [128, G * W], "float8_e4m3fn_x4"),
    "vs": ("sbuf", [128, G * W], "uint8"),
    "wq": ("sbuf", [128, N * W], "float8_e4m3fn_x4"),
    "ws": ("sbuf", [128, N * W], "uint8"),
    "pu": ("psum", [128, G * BANK], "float32"),
    "pv": ("psum", [128, G * BANK], "float32"),
    "ru": ("sbuf", [128, G * W], "float32"),
    "hb": ("sbuf", [128, E], "bfloat16"),
    "gq": ("sbuf", [128, N * W], "float8_e4m3fn_x4"),
    "gs": ("sbuf", [128, N * W], "uint8"),
    "yb": ("sbuf", [128, W], "float32"),
}
SEMAPHORES = (
    ["lx", "lu", "lv01", "lv2", "lv3", "lw"]
    + ["qx", "qu", "qv01", "qv2", "qv3", "qw", "qh"]
    + ["mu%d" % b for b in range(G)] + ["mv%d" % b for b in range(G)] + ["my"]
    + ["r%d" % b for b in range(G)] + ["hm"]
    + ["a%d" % j for j in range(N)]
    + ["ls", "cy", "sy"]
)


def some_engines(mask, count, skip=0):
    bits = [b for b in range(mask.bit_length()) if (mask >> b) & 1]
    out = 0
    for b in bits[skip:skip + count]:
        out |= 1 << b
    return out


def how_many(mask):
    return bin(mask).count("1")


def routes(T, topo):
    cores = list(T.cores)
    plan = []
    for j, src in enumerate(cores):
        near = [r for r in range(N) if r != j and topo.may_write(src, cores[r])]
        far = [r for r in range(N) if r != j and not topo.may_write(src, cores[r])]
        helpers = [c for c in range(HOSTS * topo.CORES_PER_HOST)
                   if topo.host(c) == topo.host(src) and topo.chip(c) == topo.chip(src) and T.rank_of(c) is None
                   and all(topo.may_write(c, cores[r]) for r in far)]
        helpers.sort(key=lambda c: (topo.die(c) != topo.die(src), c))
        by_codes = {r: helpers[i] for i, r in enumerate(far)}
        by_plane = {r: helpers[len(far) + i] for i, r in enumerate(far)}
        plan.append((near, far, by_codes, by_plane))
    return plan


def codes(T, j):
    return T.gq[:, W * j:W * j + W].bitcast(dt.uint8)


def plane(T, j):
    return T.gs[:, W * j:W * j + W]


def to_helpers(g, core, T, topo, j, view, helpers):
    share = how_many(topo.mask(core, helpers[0])) // len(helpers)
    transfers = []
    for i, h in enumerate(helpers):
        rid, pid = topo.addr(h, core)
        transfers.append(RemoteDMATransfer(dst_ids=[DstId(rid=rid, pnc=pid)],
                                           dma_engine_mask=some_engines(topo.mask(core, h), share, share * i),
                                           remote_sem=T.sem["a%d" % j], src=view(T, j), dst=view(T, j)))
    g.remote_dma_fused(transfers, local_sem=T.sem.ls)
    return share


def helper_share(T, topo, j, far):
    src = T.cores[j]
    plan = routes(T, topo)[j]
    return how_many(topo.mask(src, plan[2][far[0]])) // len(far)


def pass_on(g, core, T, topo, j, r, view, expected):
    dst = T.cores[r]
    rid, pid = topo.addr(dst, core)
    mask = topo.mask(core, dst)
    g.wait_ge(T.sem["a%d" % j], expected)
    g.remote_dma(view(T, j), view(T, j), T.sem["a%d" % j], T.sem.ls, pid, rid, mask)
    g.wait_ge(T.sem.ls, how_many(mask))


def rank_program(g, core, T, topo):
    plan = routes(T, topo)
    rank = T.rank_of(core)
    if rank is None:
        for j, (near, far, by_codes, by_plane) in enumerate(plan):
            for r in far:
                if by_codes[r] == core:
                    pass_on(g, core, T, topo, j, r, codes, helper_share(T, topo, j, far))
                if by_plane[r] == core:
                    pass_on(g, core, T, topo, j, r, plane, helper_share(T, topo, j, far))
        return

    S = T.sem
    near, far, by_codes, by_plane = plan[rank]
    vec, ten, act, syn = g.vector, g.tensor, g.scalar, g.sync

    syn.dma_start(T.xb[:], T.x[:]).then_inc(S.lx, 16)
    act.dma_start(T.ub[:], T.u[:]).then_inc(S.lu, 16)
    syn.dma_start(T.vb[:, 0:2 * E], T.v[:, 0:2 * E]).then_inc(S.lv01, 16)
    act.dma_start(T.vb[:, 2 * E:3 * E], T.v[:, 2 * E:3 * E]).then_inc(S.lv2, 16)
    syn.dma_start(T.vb[:, 3 * E:4 * E], T.v[:, 3 * E:4 * E]).then_inc(S.lv3, 16)
    syn.dma_start(T.wb[:], T.w2[:]).then_inc(S.lw, 16)

    def gate(b):
        vec.wait_ge(S["r%d" % b], 1)
        vec.wait_ge(S["mv%d" % b], 1)
        vec.tensor_tensor(T.hb[:, b:E:4], T.ru[:, W * b:W * b + W], T.pv[:, BANK * b:BANK * b + W],
                          AluOpType.mult).then_inc(S.hm, 1)

    vec.wait_ge(S.lx, 16)
    vec.quantize_mx(T.xq[:], T.xs[:], T.xb[:]).then_inc(S.qx, 1)
    vec.wait_ge(S.lu, 16)
    vec.quantize_mx(T.uq[:], T.us[:], T.ub[:]).then_inc(S.qu, 1)
    vec.wait_ge(S.lv01, 16)
    vec.quantize_mx(T.vq[:, 0:2 * W], T.vs[:, 0:2 * W], T.vb[:, 0:2 * E]).then_inc(S.qv01, 1)
    vec.wait_ge(S.lv2, 16)
    vec.quantize_mx(T.vq[:, 2 * W:3 * W], T.vs[:, 2 * W:3 * W], T.vb[:, 2 * E:3 * E]).then_inc(S.qv2, 1)
    gate(0)
    gate(1)
    vec.wait_ge(S.lv3, 16)
    vec.quantize_mx(T.vq[:, 3 * W:4 * W], T.vs[:, 3 * W:4 * W], T.vb[:, 3 * E:4 * E]).then_inc(S.qv3, 1)
    gate(2)
    gate(3)
    vec.wait_ge(S.hm, G)
    vec.quantize_mx(T.gq[:, W * rank:W * rank + W], T.gs[:, W * rank:W * rank + W], T.hb[:]).then_inc(S.qh, 1)
    vec.wait_ge(S.lw, 16)
    vec.quantize_mx(T.wq[:], T.ws[:], T.wb[:]).then_inc(S.qw, 1)

    def first(out, q, s, b, sem):
        ten.matmul_mx(out[:, BANK * b:BANK * b + W], q[:, W * b:W * b + W], s[:, W * b:W * b + W],
                      T.xq[:], T.xs[:], True, True).then_inc(sem, 1)

    ten.wait_ge(S.qx, 1)
    ten.wait_ge(S.qu, 1)
    for b in range(G):
        first(T.pu, T.uq, T.us, b, S["mu%d" % b])
    ten.wait_ge(S.qv01, 1)
    first(T.pv, T.vq, T.vs, 0, S.mv0)
    first(T.pv, T.vq, T.vs, 1, S.mv1)
    ten.wait_ge(S.qv2, 1)
    first(T.pv, T.vq, T.vs, 2, S.mv2)
    ten.wait_ge(S.qv3, 1)
    first(T.pv, T.vq, T.vs, 3, S.mv3)

    for b in range(G):
        act.wait_ge(S["mu%d" % b], 1)
        act.activation(T.ru[:, W * b:W * b + W], T.pu[:, BANK * b:BANK * b + W], ActivationFunctionType.Relu,
                       scale=C).then_inc(S["r%d" % b], 1)

    g.wait_ge(S.qh, 1)
    left = 0
    if far:
        left += len(far) * to_helpers(g, core, T, topo, rank, codes, [by_codes[r] for r in far])
        left += len(far) * to_helpers(g, core, T, topo, rank, plane, [by_plane[r] for r in far])
    for r in near:
        rid, pid = topo.addr(T.cores[r], core)
        mask = topo.mask(core, T.cores[r])
        for view in (codes, plane):
            g.remote_dma(view(T, rank), view(T, rank), S["a%d" % rank], S.ls, pid, rid, mask)
            left += how_many(mask)
    g.wait_ge(S.ls, left)

    order = [rank] + near + far
    ten.wait_ge(S.qh, 1)
    ten.wait_ge(S.qw, 1)
    ten.wait_ge(S.r0, 1)
    for i, j in enumerate(order):
        if j != rank:
            src = T.cores[j]
            if topo.may_write(src, core):
                expected = 2 * how_many(topo.mask(src, core))
            else:
                expected = how_many(topo.mask(plan[j][2][rank], core)) + how_many(topo.mask(plan[j][3][rank], core))
            ten.wait_ge(S["a%d" % j], expected)
        mm = ten.matmul_mx(T.pu[:, 0:W], T.wq[:, W * j:W * j + W], T.ws[:, W * j:W * j + W],
                           T.gq[:, W * j:W * j + W], T.gs[:, W * j:W * j + W], i == 0, i == len(order) - 1)
    mm.then_inc(S.my, 1)

    act.wait_ge(S.my, 1)
    act.activation(T.yb[:], T.pu[:, 0:W], ActivationFunctionType.Copy).then_inc(S.cy, 1)
    act.wait_ge(S.cy, 1)
    act.dma_start(T.y[:], T.yb[:]).then_inc(S.sy, 16)
    act.wait_ge(S.sy, 16)
